import numpy as np, ml_dtypes
CORES = [73,201,329,457,330]
N = 5
import mx_ref
NC, G = 128, 2
BF = ml_dtypes.bfloat16
def cut(t, i, w=512):
    return t[:, w * i:w * i + w]
def tile(rs):
    return np.stack(rs, axis=2).reshape(128, -1).astype(BF)
def layer(w, X):
    out = []
    for i in range(G):
        for t in range(len(X)):
            p = mx_ref.matmul(mx_ref.quantize(cut(w, len(X) * i + t)), X[t])
            z = p if t == 0 else z + p
        out.append(z)
    return out
def scaled(Z, s):
    return [np.maximum(k * z, 0) * s for z in Z for k in (1, -1)]
def setup_inputs(rng):
    def f(*shape):
        return mx_ref.flush((rng.standard_normal(shape, dtype=np.float32) * np.exp2(rng.integers(-2, 3, shape[:-1] + (1,)))).astype(BF))
    return {"x": f(N, 128, 4 * NC), "w1": f(N, 128, G * 512), "w2": f(N, 128, 2 * 512)}
def setup_inputs_blocks(rng):
    d = setup_inputs(rng)
    for k in ("w2",): d[k] = mx_ref.spread(d[k], rng, 4)
    for k in ("x", "w1"): d[k] = mx_ref.spread(d[k], rng, 2)
    return d
def setup_inputs_wide(rng):
    d = setup_inputs(rng)
    for k in ("x", "w1", "w2"): d[k] = mx_ref.flush((d[k].astype(np.float32) * np.exp2(rng.integers(-3, 4, (N, 1, 1))).astype(np.float32)).astype(BF))
    return d
def reference(x, w1, w2, own=None):
    Z = [layer(w1[r], [mx_ref.quantize(x[r])]) for r in range(N)]
    a = max(float(np.abs(z).max()) for r in range(N) for z in Z[r])
    s = np.float32(1 / a)
    h = np.stack([tile(scaled(Z[r], s)) for r in range(N)])
    use = h if own is None else own["h"]
    H = [mx_ref.quantize(use[j]) for j in range(N)]
    y = np.zeros((N, 128, NC), np.float32)
    for r in range(N):
        y[r] = mx_ref.matmul(mx_ref.quantize(cut(w2[r], 0)), H[r]) + mx_ref.matmul(mx_ref.quantize(cut(w2[r], 1)), H[(r + 1) % N])
    return {"h": h, "y": y}

@@ -1,0 +1,228 @@
+from concourse.bass import DstId, RemoteDMATransfer
+from concourse.mybir import dt, AluOpType, AxisListType, ActivationFunctionType
+
+NC = 128
+OWN = 3
+BANK = 512
+
+SCRATCH = {
+    "xt": ("sbuf", [128, 4 * NC], "bfloat16"),
+    "w1t": ("sbuf", [128, 8 * NC], "bfloat16"),
+    "w2t": ("sbuf", [128, 8 * NC], "bfloat16"),
+    "qx": ("sbuf", [128, NC], "float8_e4m3fn_x4"),
+    "sx": ("sbuf", [128, NC], "uint8"),
+    "qw1": ("sbuf", [128, 2 * NC], "float8_e4m3fn_x4"),
+    "sw1": ("sbuf", [128, 2 * NC], "uint8"),
+    "qw2": ("sbuf", [128, 2 * NC], "float8_e4m3fn_x4"),
+    "sw2": ("sbuf", [128, 2 * NC], "uint8"),
+    "zero": ("sbuf", [128, NC], "float32"),
+    "one": ("sbuf", [128, NC], "float32"),
+    "ident": ("sbuf", [128, NC], "float32"),
+    "m": ("sbuf", [128, 4], "float32"),
+    "mb": ("sbuf", [128, NC], "float32"),
+    "g": ("sbuf", [128, 8], "float32"),
+    "a": ("sbuf", [128, 4], "float32"),
+    "s": ("sbuf", [128, 4], "float32"),
+    "e": ("sbuf", [128, 4 * NC], "float32"),
+    "ht": ("sbuf", [128, 4 * NC], "bfloat16"),
+    "qh": ("sbuf", [128, NC], "float8_e4m3fn_x4"),
+    "sh": ("sbuf", [128, NC], "uint8"),
+    "qn": ("sbuf", [128, NC], "float8_e4m3fn_x4"),
+    "sn": ("sbuf", [128, NC], "uint8"),
+    "qr": ("sbuf", [128, NC], "float8_e4m3fn_x4"),
+    "sr": ("sbuf", [128, NC], "uint8"),
+    "yt": ("sbuf", [128, NC], "float32"),
+    "z": ("psum", [128, 2 * BANK], "float32"),
+    "pt": ("psum", [128, BANK], "float32"),
+    "yp": ("psum", [128, BANK], "float32"),
+}
+SEMAPHORES = ["lx", "lw0", "lw1", "lw2", "c0", "c1", "ci", "vqx", "vq0", "vq1", "vq2", "tz0", "tz1", "vm0", "vm1", "vb", "tp",
+              "own", "ev", "es", "va", "vs", "hv", "hs", "vh", "ty", "vy", "sth", "sty",
+              "peer", "cross", "hin", "rel", "left", "lefth"]
+
+
+def engines(mask):
+    return bin(mask).count("1")
+
+
+def rack_of(topo, core):
+    return topo.rack(topo.host(core))
+
+
+def columns(T, topo, r):
+    cores = T.cores
+    return [r] + [q for q in range(len(cores)) if q != r and rack_of(topo, cores[q]) == rack_of(topo, cores[r])]
+
+
+def gate(T, topo, r):
+    cores = T.cores
+    return [q for q in range(len(cores)) if rack_of(topo, cores[q]) != rack_of(topo, cores[r]) and topo.may_write(cores[q], cores[r])][0]
+
+
+def relays(T, topo, r, reader):
+    cores = T.cores
+    if topo.may_write(cores[r], cores[reader]):
+        return []
+    via = [q for q in range(len(cores)) if q not in (r, reader) and topo.may_write(cores[r], cores[q]) and topo.may_write(cores[q], cores[reader])]
+    via.sort(key=lambda q: (rack_of(topo, cores[q]) != rack_of(topo, cores[r]), q))
+    return [via[0], via[-1]]
+
+
+def rank_program(g, core, T, topo):
+    rank = T.rank_of(core)
+    if rank is None:
+        return
+    cores = T.cores
+    n = len(cores)
+    S = T.sem
+    V, X, P, Y = g.vector, g.scalar, g.tensor, g.sync
+    MAX, MULT = AluOpType.max, AluOpType.mult
+    Relu, Copy = ActivationFunctionType.Relu, ActivationFunctionType.Copy
+    H = 2 * NC
+    left = [0]
+
+    def send(pairs, src, remote_sem, local_sem, mask):
+        if local_sem is S.left:
+            left[0] += engines(mask)
+        if len(pairs) == 1:
+            rid, pid = topo.addr(pairs[0][0], core)
+            g.remote_dma(pairs[0][1], src, remote_sem, local_sem, pid, rid, mask)
+            return
+        ids = []
+        for d, _ in pairs:
+            rid, pid = topo.addr(d, core)
+            ids.append(DstId(rid=rid, pnc=pid))
+        g.remote_dma_fused([RemoteDMATransfer(dst_ids=ids, dma_engine_mask=mask, remote_sem=remote_sem,
+                                              srcs=[src], dsts=[ap for _, ap in pairs])], local_sem=local_sem)
+
+    mine = columns(T, topo, rank)
+    peers = mine[1:]
+    far = [q for q in peers if topo.host(cores[q]) != topo.host(core)]
+    near = [q for q in peers if q not in far]
+    served = [q for q in range(n) if gate(T, topo, q) == rank]
+    reader = (rank - 1) % n
+    via = relays(T, topo, rank, reader)
+    out_mask = topo.mask(core, cores[(far + served)[0]])
+    for q in range(n):
+        if q != rank and topo.may_write(core, cores[q]):
+            out_mask &= topo.mask(core, cores[q])
+    ne = engines(out_mask)
+
+    Y.dma_start(T.xt[:], T.x[:]).then_inc(S.lx, 16)
+    X.dma_start(T.w1t[:, 0:4 * NC], T.w1[:, 0:4 * NC]).then_inc(S.lw0, 16)
+    Y.dma_start(T.w1t[:, 4 * NC:8 * NC], T.w1[:, 4 * NC:8 * NC]).then_inc(S.lw1, 16)
+    Y.wait_ge(S.lw1, 16)
+    Y.dma_start(T.w2t[:], T.w2[:]).then_inc(S.lw2, 16)
+
+    V.memset(T.one[:], 1.0).then_inc(S.c1, 1)
+    V.memset(T.zero[:], 0.0).then_inc(S.c0, 1)
+    g.wait_ge(S.c1, 1)
+    g.affine_select(T.ident[:], T.one[:], [[-1, NC]], AluOpType.is_equal, 0.0, 0, 1).then_inc(S.ci, 1)
+
+    V.wait_ge(S.lx, 16)
+    V.quantize_mx(T.qx[:], T.sx[:], T.xt[:]).then_inc(S.vqx, 1)
+    V.wait_ge(S.lw0, 16)
+    V.quantize_mx(T.qw1[:, 0:NC], T.sw1[:, 0:NC], T.w1t[:, 0:4 * NC]).then_inc(S.vq0, 1)
+    V.wait_ge(S.lw1, 16)
+    V.quantize_mx(T.qw1[:, NC:2 * NC], T.sw1[:, NC:2 * NC], T.w1t[:, 4 * NC:8 * NC]).then_inc(S.vq1, 1)
+    z0, z1 = T.z[:, 0:NC], T.z[:, BANK:BANK + NC]
+    P.wait_ge(S.vqx, 1)
+    P.wait_ge(S.vq0, 1)
+    P.matmul_mx(z0, T.qw1[:, 0:NC], T.sw1[:, 0:NC], T.qx[:], T.sx[:], True, True).then_inc(S.tz0, 1)
+    P.wait_ge(S.vq1, 1)
+    P.matmul_mx(z1, T.qw1[:, NC:2 * NC], T.sw1[:, NC:2 * NC], T.qx[:], T.sx[:], True, True).then_inc(S.tz1, 1)
+
+    V.wait_ge(S.tz0, 1)
+    V.tensor_reduce(T.m[:, 0:1], z0, AxisListType.X, MAX, apply_absolute_value=True).then_inc(S.vm0, 1)
+    V.wait_ge(S.tz1, 1)
+    V.tensor_reduce(T.m[:, 1:2], z1, AxisListType.X, MAX, apply_absolute_value=True).then_inc(S.vm1, 1)
+    V.wait_ge(S.c0, 1)
+    V.wait_ge(S.vm0, 1)
+    V.wait_ge(S.vm1, 1)
+    V.tensor_scalar(T.mb[:], T.zero[:], T.m[:, 0:1], T.m[:, 1:2], MAX, MAX).then_inc(S.vb, 1)
+    P.wait_ge(S.ci, 1)
+    P.wait_ge(S.vb, 1)
+    P.matmul(T.pt[:, 0:NC], T.mb[:], T.ident[:], True, True).then_inc(S.tp, 1)
+    V.wait_ge(S.tp, 1)
+    V.tensor_reduce(T.g[:, OWN:OWN + 1], T.pt[:, 0:NC], AxisListType.X, MAX).then_inc(S.own, 1)
+
+    g.wait_ge(S.own, 1)
+    for dests in (far, near):
+        if dests:
+            pairs = []
+            for q in dests:
+                c = OWN + columns(T, topo, q).index(rank)
+                pairs.append((cores[q], T.g[:, c:c + 1]))
+            send(pairs, T.g[:, OWN:OWN + 1], S.peer, S.left, out_mask)
+    if served:
+        g.wait_ge(S.peer, ne * len(peers))
+        pairs = []
+        for q in served:
+            c = OWN + len(columns(T, topo, q))
+            pairs.append((cores[q], T.g[:, c:c + len(mine)]))
+        send(pairs, T.g[:, OWN:OWN + len(mine)], S.cross, S.left, out_mask)
+
+    V.tensor_scalar(T.e[:, 0:4 * NC:4], z0, 0.0, None, MAX).then_inc(S.ev, 1)
+    V.tensor_scalar(T.e[:, 1:4 * NC:4], z0, -1.0, 0.0, MULT, MAX).then_inc(S.ev, 1)
+    X.wait_ge(S.vm1, 1)
+    X.activation(T.e[:, 2:4 * NC:4], z1, Relu, scale=1.0).then_inc(S.es, 1)
+    X.activation(T.e[:, 3:4 * NC:4], z1, Relu, scale=-1.0).then_inc(S.es, 1)
+    V.wait_ge(S.lw2, 16)
+    V.quantize_mx(T.qw2[:], T.sw2[:], T.w2t[:]).then_inc(S.vq2, 1)
+
+    V.wait_ge(S.ev, 2)
+    V.wait_ge(S.es, 2)
+    V.wait_ge(S.own, 1)
+    V.wait_ge(S.peer, ne * len(peers))
+    V.wait_ge(S.cross, ne)
+    V.tensor_reduce(T.a[:, 0:1], T.g[:, OWN:OWN + n], AxisListType.X, MAX).then_inc(S.va, 1)
+    V.wait_ge(S.va, 1)
+    V.reciprocal(T.s[:, 0:1], T.a[:, 0:1]).then_inc(S.vs, 1)
+    V.wait_ge(S.vs, 1)
+    V.tensor_scalar(T.ht[:, 0:H], T.e[:, 0:H], T.s[:, 0:1], None, MULT).then_inc(S.hv, 1)
+    X.wait_ge(S.ev, 2)
+    X.wait_ge(S.es, 2)
+    X.wait_ge(S.vs, 1)
+    X.activation(T.ht[:, H:2 * H], T.e[:, H:2 * H], Copy, scale=T.s[:, 0:1]).then_inc(S.hs, 1)
+    V.wait_ge(S.hv, 1)
+    V.wait_ge(S.hs, 1)
+    V.quantize_mx(T.qh[:], T.sh[:], T.ht[:]).then_inc(S.vh, 1)
+
+    codes, scales = T.qh[:, 0:NC].bitcast(dt.uint8), T.sh[:, 0:NC]
+    g.wait_ge(S.vh, 1)
+    if via:
+        send([(cores[via[0]], T.qr[:, 0:NC].bitcast(dt.uint8))], codes, S.rel, S.lefth, out_mask)
+        send([(cores[via[1]], T.sr[:, 0:NC])], scales, S.rel, S.lefth, out_mask)
+    else:
+        send([(cores[reader], T.qn[:, 0:NC].bitcast(dt.uint8))], codes, S.hin, S.lefth, out_mask)
+        send([(cores[reader], T.sn[:, 0:NC])], scales, S.hin, S.lefth, out_mask)
+    for src in range(n):
+        end = (src - 1) % n
+        over = relays(T, topo, src, end)
+        if over and over[0] == rank:
+            g.wait_ge(S.rel, ne)
+            send([(cores[end], T.qn[:, 0:NC].bitcast(dt.uint8))], T.qr[:, 0:NC].bitcast(dt.uint8), S.hin, S.left, out_mask)
+        if over and over[1] == rank:
+            g.wait_ge(S.rel, ne)
+            send([(cores[end], T.sn[:, 0:NC])], T.sr[:, 0:NC], S.hin, S.left, out_mask)
+
+    Y.wait_ge(S.hv, 1)
+    Y.wait_ge(S.hs, 1)
+    if via:
+        Y.wait_ge(S.lefth, 2 * ne)
+    Y.dma_start(T.h[:], T.ht[:]).then_inc(S.sth, 16)
+
+    P.wait_ge(S.vq2, 1)
+    P.wait_ge(S.vh, 1)
+    P.matmul_mx(T.yp[:, 0:NC], T.qw2[:, 0:NC], T.sw2[:, 0:NC], T.qh[:], T.sh[:], True, False)
+    P.wait_ge(S.hin, 2 * ne)
+    P.matmul_mx(T.yp[:, 0:NC], T.qw2[:, NC:2 * NC], T.sw2[:, NC:2 * NC], T.qn[:], T.sn[:], False, True).then_inc(S.ty, 1)
+    V.wait_ge(S.ty, 1)
+    V.tensor_copy(T.yt[:], T.yp[:, 0:NC]).then_inc(S.vy, 1)
+    Y.wait_ge(S.vy, 1)
+    Y.dma_start(T.y[:], T.yt[:]).then_inc(S.sty, 16)
+
+    g.wait_ge(S.left, left[0])
+    g.wait_ge(S.lefth, 2 * ne)
+    Y.wait_ge(S.sth, 16)
+    Y.wait_ge(S.sty, 16)

@@ -4,6 +4,7 @@ from concourse.mybir import dt, AluOpType, AxisListType, ActivationFunctionType
 NC = 128
 OWN = 3
 BANK = 512
+CUT = 96
 
 SCRATCH = {
     "xt": ("sbuf", [128, 4 * NC], "bfloat16"),
@@ -38,11 +39,16 @@ SCRATCH = {
 }
 SEMAPHORES = ["lx", "lw0", "lw1", "lw2", "c0", "c1", "ci", "vqx", "vq0", "vq1", "vq2", "tz0", "tz1", "vm0", "vm1", "vb", "tp",
               "own", "ev", "es", "va", "vs", "hv", "hs", "vh", "ty", "vy", "sth", "sty",
-              "peer", "cross", "hin", "rel", "left", "lefth"]
+              "peer1", "peer2", "cross", "hin", "rel", "left", "lefth"]
 
 
 def engines(mask):
     return bin(mask).count("1")
+
+
+def some(mask, first, k):
+    bits = [b for b in range(mask.bit_length()) if mask >> b & 1]
+    return sum(1 << b for b in bits[first:first + k])
 
 
 def rack_of(topo, core):
@@ -54,9 +60,20 @@ def columns(T, topo, r):
     return [r] + [q for q in range(len(cores)) if q != r and rack_of(topo, cores[q]) == rack_of(topo, cores[r])]
 
 
-def gate(T, topo, r):
+def calls_to_peers(T, topo, r):
     cores = T.cores
-    return [q for q in range(len(cores)) if rack_of(topo, cores[q]) != rack_of(topo, cores[r]) and topo.may_write(cores[q], cores[r])][0]
+    peers = columns(T, topo, r)[1:]
+    away = [q for q in peers if topo.host(cores[q]) != topo.host(cores[r])]
+    return [away, [q for q in peers if q not in away]]
+
+
+def across(T, topo, r):
+    cores = T.cores
+    other = [q for q in range(len(cores)) if rack_of(topo, cores[q]) != rack_of(topo, cores[r])]
+    able = [q for q in other if topo.may_write(cores[q], cores[r])]
+    held = columns(T, topo, able[0])
+    k = max([0] + [held.index(q) for q in other if q not in able]) + 1
+    return [(able[0], k)] + [(q, 1) for q in able[1:] if q not in held[:k]]
 
 
 def relays(T, topo, r, reader):
@@ -66,6 +83,14 @@ def relays(T, topo, r, reader):
     via = [q for q in range(len(cores)) if q not in (r, reader) and topo.may_write(cores[r], cores[q]) and topo.may_write(cores[q], cores[reader])]
     via.sort(key=lambda q: (rack_of(topo, cores[q]) != rack_of(topo, cores[r]), q))
     return [via[0], via[-1]]
+
+
+def wide(T, topo, r):
+    masks = [topo.mask(T.cores[r], c) for c in T.cores if c != T.cores[r] and topo.may_write(T.cores[r], c)]
+    m = masks[0]
+    for k in masks:
+        m &= k
+    return m
 
 
 def rank_program(g, core, T, topo):
@@ -79,34 +104,45 @@ def rank_program(g, core, T, topo):
     MAX, MULT = AluOpType.max, AluOpType.mult
     Relu, Copy = ActivationFunctionType.Relu, ActivationFunctionType.Copy
     H = 2 * NC
-    left = [0]
+    left = {"left": 0, "lefth": 0}
+    mask = wide(T, topo, rank)
 
-    def send(pairs, src, remote_sem, local_sem, mask):
-        if local_sem is S.left:
-            left[0] += engines(mask)
-        if len(pairs) == 1:
-            rid, pid = topo.addr(pairs[0][0], core)
-            g.remote_dma(pairs[0][1], src, remote_sem, local_sem, pid, rid, mask)
-            return
-        ids = []
-        for d, _ in pairs:
+    def send(parts, local):
+        left[local] += engines(mask)
+        if len(parts) == 1 and len(parts[0][2]) == 1:
+            src, sem, [(d, out)] = parts[0]
             rid, pid = topo.addr(d, core)
-            ids.append(DstId(rid=rid, pnc=pid))
-        g.remote_dma_fused([RemoteDMATransfer(dst_ids=ids, dma_engine_mask=mask, remote_sem=remote_sem,
-                                              srcs=[src], dsts=[ap for _, ap in pairs])], local_sem=local_sem)
+            g.remote_dma(out, src, sem, S[local], pid, rid, mask)
+            return
+        k = engines(mask) // len(parts)
+        ts = []
+        for i, (src, sem, dests) in enumerate(parts):
+            ids = []
+            for d, _ in dests:
+                rid, pid = topo.addr(d, core)
+                ids.append(DstId(rid=rid, pnc=pid))
+            ts.append(RemoteDMATransfer(dst_ids=ids, dma_engine_mask=some(mask, i * k, k), remote_sem=sem,
+                                        srcs=[src], dsts=[out for _, out in dests]))
+        g.remote_dma_fused(ts, local_sem=S[local])
+
+    def codes(t, a, b):
+        return t[:, a:b].bitcast(dt.uint8)
+
+    def col(c, k=1):
+        return T.g[:, c:c + k]
 
     mine = columns(T, topo, rank)
-    peers = mine[1:]
-    far = [q for q in peers if topo.host(cores[q]) != topo.host(core)]
-    near = [q for q in peers if q not in far]
-    served = [q for q in range(n) if gate(T, topo, q) == rank]
     reader = (rank - 1) % n
+    source = (rank + 1) % n
     via = relays(T, topo, rank, reader)
-    out_mask = topo.mask(core, cores[(far + served)[0]])
-    for q in range(n):
-        if q != rank and topo.may_write(core, cores[q]):
-            out_mask &= topo.mask(core, cores[q])
-    ne = engines(out_mask)
+
+    def peer_sem(r, q):
+        return S["peer%d" % columns(T, topo, r).index(q)]
+
+    def wait_peers(queue, which):
+        for q in which:
+            together = [len(c) for c in calls_to_peers(T, topo, q) if rank in c][0]
+            queue.wait_ge(peer_sem(rank, q), engines(wide(T, topo, q)) // together)
 
     Y.dma_start(T.xt[:], T.x[:]).then_inc(S.lx, 16)
     X.dma_start(T.w1t[:, 0:4 * NC], T.w1[:, 0:4 * NC]).then_inc(S.lw0, 16)
@@ -144,23 +180,32 @@ def rank_program(g, core, T, topo):
     P.wait_ge(S.vb, 1)
     P.matmul(T.pt[:, 0:NC], T.mb[:], T.ident[:], True, True).then_inc(S.tp, 1)
     V.wait_ge(S.tp, 1)
-    V.tensor_reduce(T.g[:, OWN:OWN + 1], T.pt[:, 0:NC], AxisListType.X, MAX).then_inc(S.own, 1)
+    V.tensor_reduce(col(OWN), T.pt[:, 0:NC], AxisListType.X, MAX).then_inc(S.own, 1)
+
+    def to_peers(which):
+        if which:
+            send([(col(OWN), peer_sem(q, rank), [(cores[q], col(OWN + columns(T, topo, q).index(rank)))]) for q in which], "left")
+
+    def to_other_rack(single):
+        groups = {}
+        for q in range(n):
+            at = OWN + len(columns(T, topo, q))
+            if rack_of(topo, cores[q]) == rack_of(topo, core):
+                continue
+            for s, k in across(T, topo, q):
+                if s == rank and (k == 1) == single:
+                    groups.setdefault(k, []).append((cores[q], col(at, k)))
+                at += k
+        for k in groups:
+            wait_peers(g, mine[1:k])
+            send([(col(OWN, k), S.cross, groups[k])], "left")
 
     g.wait_ge(S.own, 1)
-    for dests in (far, near):
-        if dests:
-            pairs = []
-            for q in dests:
-                c = OWN + columns(T, topo, q).index(rank)
-                pairs.append((cores[q], T.g[:, c:c + 1]))
-            send(pairs, T.g[:, OWN:OWN + 1], S.peer, S.left, out_mask)
-    if served:
-        g.wait_ge(S.peer, ne * len(peers))
-        pairs = []
-        for q in served:
-            c = OWN + len(columns(T, topo, q))
-            pairs.append((cores[q], T.g[:, c:c + len(mine)]))
-        send(pairs, T.g[:, OWN:OWN + len(mine)], S.cross, S.left, out_mask)
+    other_chip, same_chip = calls_to_peers(T, topo, rank)
+    to_peers(other_chip)
+    to_other_rack(True)
+    to_peers(same_chip)
+    to_other_rack(False)
 
     V.tensor_scalar(T.e[:, 0:4 * NC:4], z0, 0.0, None, MAX).then_inc(S.ev, 1)
     V.tensor_scalar(T.e[:, 1:4 * NC:4], z0, -1.0, 0.0, MULT, MAX).then_inc(S.ev, 1)
@@ -173,9 +218,9 @@ def rank_program(g, core, T, topo):
     V.wait_ge(S.ev, 2)
     V.wait_ge(S.es, 2)
     V.wait_ge(S.own, 1)
-    V.wait_ge(S.peer, ne * len(peers))
-    V.wait_ge(S.cross, ne)
-    V.tensor_reduce(T.a[:, 0:1], T.g[:, OWN:OWN + n], AxisListType.X, MAX).then_inc(S.va, 1)
+    wait_peers(V, mine[1:])
+    V.wait_ge(S.cross, sum(engines(wide(T, topo, q)) for q, _ in across(T, topo, rank)))
+    V.tensor_reduce(T.a[:, 0:1], col(OWN, n), AxisListType.X, MAX).then_inc(S.va, 1)
     V.wait_ge(S.va, 1)
     V.reciprocal(T.s[:, 0:1], T.a[:, 0:1]).then_inc(S.vs, 1)
     V.wait_ge(S.vs, 1)
@@ -188,41 +233,45 @@ def rank_program(g, core, T, topo):
     V.wait_ge(S.hs, 1)
     V.quantize_mx(T.qh[:], T.sh[:], T.ht[:]).then_inc(S.vh, 1)
 
-    codes, scales = T.qh[:, 0:NC].bitcast(dt.uint8), T.sh[:, 0:NC]
     g.wait_ge(S.vh, 1)
     if via:
-        send([(cores[via[0]], T.qr[:, 0:NC].bitcast(dt.uint8))], codes, S.rel, S.lefth, out_mask)
-        send([(cores[via[1]], T.sr[:, 0:NC])], scales, S.rel, S.lefth, out_mask)
+        first, second = cores[via[0]], cores[via[1]]
+        send([(codes(T.qh, 0, CUT), S.rel, [(first, codes(T.qr, 0, CUT))])], "lefth")
+        send([(T.sh[:, 0:NC], S.rel, [(second, T.sr[:, 0:NC])]),
+              (codes(T.qh, CUT, NC), S.rel, [(second, codes(T.qr, CUT, NC))])], "lefth")
     else:
-        send([(cores[reader], T.qn[:, 0:NC].bitcast(dt.uint8))], codes, S.hin, S.lefth, out_mask)
-        send([(cores[reader], T.sn[:, 0:NC])], scales, S.hin, S.lefth, out_mask)
+        send([(codes(T.qh, 0, NC), S.hin, [(cores[reader], codes(T.qn, 0, NC))])], "lefth")
+        send([(T.sh[:, 0:NC], S.hin, [(cores[reader], T.sn[:, 0:NC])])], "lefth")
     for src in range(n):
         end = (src - 1) % n
         over = relays(T, topo, src, end)
-        if over and over[0] == rank:
-            g.wait_ge(S.rel, ne)
-            send([(cores[end], T.qn[:, 0:NC].bitcast(dt.uint8))], T.qr[:, 0:NC].bitcast(dt.uint8), S.hin, S.left, out_mask)
-        if over and over[1] == rank:
-            g.wait_ge(S.rel, ne)
-            send([(cores[end], T.sn[:, 0:NC])], T.sr[:, 0:NC], S.hin, S.left, out_mask)
+        if rank not in over:
+            continue
+        g.wait_ge(S.rel, engines(wide(T, topo, src)))
+        if over[0] == rank:
+            send([(codes(T.qr, 0, CUT), S.hin, [(cores[end], codes(T.qn, 0, CUT))])], "left")
+        else:
+            send([(T.sr[:, 0:NC], S.hin, [(cores[end], T.sn[:, 0:NC])]),
+                  (codes(T.qr, CUT, NC), S.hin, [(cores[end], codes(T.qn, CUT, NC))])], "left")
 
     Y.wait_ge(S.hv, 1)
     Y.wait_ge(S.hs, 1)
     if via:
-        Y.wait_ge(S.lefth, 2 * ne)
+        Y.wait_ge(S.lefth, left["lefth"])
     Y.dma_start(T.h[:], T.ht[:]).then_inc(S.sth, 16)
 
     P.wait_ge(S.vq2, 1)
     P.wait_ge(S.vh, 1)
     P.matmul_mx(T.yp[:, 0:NC], T.qw2[:, 0:NC], T.sw2[:, 0:NC], T.qh[:], T.sh[:], True, False)
-    P.wait_ge(S.hin, 2 * ne)
+    over = relays(T, topo, source, rank)
+    P.wait_ge(S.hin, sum(engines(wide(T, topo, q)) for q in over) or 2 * engines(wide(T, topo, source)))
     P.matmul_mx(T.yp[:, 0:NC], T.qw2[:, NC:2 * NC], T.sw2[:, NC:2 * NC], T.qn[:], T.sn[:], False, True).then_inc(S.ty, 1)
     V.wait_ge(S.ty, 1)
     V.tensor_copy(T.yt[:], T.yp[:, 0:NC]).then_inc(S.vy, 1)
     Y.wait_ge(S.vy, 1)
     Y.dma_start(T.y[:], T.yt[:]).then_inc(S.sty, 16)
 
-    g.wait_ge(S.left, left[0])
-    g.wait_ge(S.lefth, 2 * ne)
+    g.wait_ge(S.left, left["left"])
+    g.wait_ge(S.lefth, left["lefth"])
     Y.wait_ge(S.sth, 16)
     Y.wait_ge(S.sty, 16)

@@ -2,9 +2,10 @@ from concourse.bass import DstId, RemoteDMATransfer
 from concourse.mybir import dt, AluOpType, AxisListType, ActivationFunctionType
 
 NC = 128
-OWN = 3
+FIRST = 3
 BANK = 512
-CUT = 96
+CUT = 80
+HEAD = 48
 
 SCRATCH = {
     "xt": ("sbuf", [128, 4 * NC], "bfloat16"),
@@ -19,8 +20,11 @@ SCRATCH = {
     "zero": ("sbuf", [128, NC], "float32"),
     "one": ("sbuf", [128, NC], "float32"),
     "ident": ("sbuf", [128, NC], "float32"),
-    "m": ("sbuf", [128, 4], "float32"),
+    "m": ("sbuf", [128, 8], "float32"),
     "mb": ("sbuf", [128, NC], "float32"),
+    "mc": ("sbuf", [128, NC], "float32"),
+    "md": ("sbuf", [128, NC], "float32"),
+    "ah": ("sbuf", [128, 4], "float32"),
     "g": ("sbuf", [128, 8], "float32"),
     "a": ("sbuf", [128, 4], "float32"),
     "s": ("sbuf", [128, 4], "float32"),
@@ -34,21 +38,23 @@ SCRATCH = {
     "sr": ("sbuf", [128, NC], "uint8"),
     "yt": ("sbuf", [128, NC], "float32"),
     "z": ("psum", [128, 2 * BANK], "float32"),
-    "pt": ("psum", [128, BANK], "float32"),
+    "pb": ("psum", [128, BANK], "float32"),
+    "pc": ("psum", [128, BANK], "float32"),
+    "pd": ("psum", [128, BANK], "float32"),
     "yp": ("psum", [128, BANK], "float32"),
 }
-SEMAPHORES = ["lx", "lw0", "lw1", "lw2", "c0", "c1", "ci", "vqx", "vq0", "vq1", "vq2", "tz0", "tz1", "vm0", "vm1", "vb", "tp",
-              "own", "ev", "es", "va", "vs", "hv", "hs", "vh", "ty", "vy", "sth", "sty",
-              "peer1", "peer2", "cross", "hin", "rel", "left", "lefth"]
+SEMAPHORES = ["lx", "lw0", "lw1", "lw2", "c0", "c1", "ci", "vqx", "vq0", "vq1", "vq2", "tz0", "tz1", "vm0", "vm1",
+              "vb", "tb", "own", "vc", "tc", "late", "vd", "td", "early", "es", "va", "vs", "hv", "hs", "vh", "ty", "vy",
+              "sth", "sty", "ahead", "peer1", "peer2", "cross", "hin", "rel1", "rel2", "help", "left", "lefth"]
 
 
 def engines(mask):
     return bin(mask).count("1")
 
 
-def some(mask, first, k):
+def share(mask, i, k):
     bits = [b for b in range(mask.bit_length()) if mask >> b & 1]
-    return sum(1 << b for b in bits[first:first + k])
+    return sum(1 << b for b in bits[i::k])
 
 
 def rack_of(topo, core):
@@ -85,6 +91,23 @@ def relays(T, topo, r, reader):
     return [via[0], via[-1]]
 
 
+def helper(T, topo, r, reader):
+    cores = T.cores
+    if relays(T, topo, r, reader) or rack_of(topo, cores[r]) == rack_of(topo, cores[reader]):
+        return None
+    near = [q for q in range(len(cores)) if q not in (r, reader) and topo.host(cores[q]) == topo.host(cores[r]) and topo.may_write(cores[q], cores[reader])]
+    return near[0] if near else None
+
+
+def targets(T, topo, r):
+    return [q for q in range(len(T.cores)) if rack_of(topo, T.cores[q]) != rack_of(topo, T.cores[r]) and r in [s for s, _ in across(T, topo, q)]]
+
+
+def ahead(T, topo, r):
+    to = targets(T, topo, r)
+    return [] if any(relays(T, topo, q, (q - 1) % len(T.cores)) for q in to) else to
+
+
 def wide(T, topo, r):
     masks = [topo.mask(T.cores[r], c) for c in T.cores if c != T.cores[r] and topo.may_write(T.cores[r], c)]
     m = masks[0]
@@ -114,14 +137,13 @@ def rank_program(g, core, T, topo):
             rid, pid = topo.addr(d, core)
             g.remote_dma(out, src, sem, S[local], pid, rid, mask)
             return
-        k = engines(mask) // len(parts)
         ts = []
         for i, (src, sem, dests) in enumerate(parts):
             ids = []
             for d, _ in dests:
                 rid, pid = topo.addr(d, core)
                 ids.append(DstId(rid=rid, pnc=pid))
-            ts.append(RemoteDMATransfer(dst_ids=ids, dma_engine_mask=some(mask, i * k, k), remote_sem=sem,
+            ts.append(RemoteDMATransfer(dst_ids=ids, dma_engine_mask=share(mask, i, len(parts)), remote_sem=sem,
                                         srcs=[src], dsts=[out for _, out in dests]))
         g.remote_dma_fused(ts, local_sem=S[local])
 
@@ -135,6 +157,10 @@ def rank_program(g, core, T, topo):
     reader = (rank - 1) % n
     source = (rank + 1) % n
     via = relays(T, topo, rank, reader)
+    to_ahead = ahead(T, topo, rank)
+    from_ahead = [q for q in range(n) if rank in ahead(T, topo, q)]
+    OWN = FIRST - 1 if to_ahead else FIRST
+    EARLY = OWN - 1 if from_ahead else OWN
 
     def peer_sem(r, q):
         return S["peer%d" % columns(T, topo, r).index(q)]
@@ -147,7 +173,7 @@ def rank_program(g, core, T, topo):
     Y.dma_start(T.xt[:], T.x[:]).then_inc(S.lx, 16)
     X.dma_start(T.w1t[:, 0:4 * NC], T.w1[:, 0:4 * NC]).then_inc(S.lw0, 16)
     Y.dma_start(T.w1t[:, 4 * NC:8 * NC], T.w1[:, 4 * NC:8 * NC]).then_inc(S.lw1, 16)
-    Y.wait_ge(S.lw1, 16)
+    wait_peers(Y, mine[1:])
     Y.dma_start(T.w2t[:], T.w2[:]).then_inc(S.lw2, 16)
 
     V.memset(T.one[:], 1.0).then_inc(S.c1, 1)
@@ -168,28 +194,38 @@ def rank_program(g, core, T, topo):
     P.wait_ge(S.vq1, 1)
     P.matmul_mx(z1, T.qw1[:, NC:2 * NC], T.sw1[:, NC:2 * NC], T.qx[:], T.sx[:], True, True).then_inc(S.tz1, 1)
 
+    m0, m1 = T.m[:, 0:1], T.m[:, 4:5]
     V.wait_ge(S.tz0, 1)
-    V.tensor_reduce(T.m[:, 0:1], z0, AxisListType.X, MAX, apply_absolute_value=True).then_inc(S.vm0, 1)
+    V.tensor_reduce(m0, z0, AxisListType.X, MAX, apply_absolute_value=True).then_inc(S.vm0, 1)
     V.wait_ge(S.tz1, 1)
-    V.tensor_reduce(T.m[:, 1:2], z1, AxisListType.X, MAX, apply_absolute_value=True).then_inc(S.vm1, 1)
+    V.tensor_reduce(m1, z1, AxisListType.X, MAX, apply_absolute_value=True).then_inc(S.vm1, 1)
+
+    def over_partitions(out, parts, spread, turned, v, t, done, meanwhile=None):
+        if len(parts) == 2:
+            V.tensor_scalar(spread[:], T.zero[:], parts[0], parts[1], MAX, MAX).then_inc(v, 1)
+        else:
+            V.tensor_scalar(spread[:], T.zero[:], parts[0], None, MAX).then_inc(v, 1)
+        P.wait_ge(v, 1)
+        P.matmul(turned[:, 0:NC], spread[:], T.ident[:], True, True).then_inc(t, 1)
+        V.wait_ge(t, 1)
+        V.tensor_reduce(out, turned[:, 0:NC], AxisListType.X, MAX).then_inc(done, 1)
+
     V.wait_ge(S.c0, 1)
     V.wait_ge(S.vm0, 1)
     V.wait_ge(S.vm1, 1)
-    V.tensor_scalar(T.mb[:], T.zero[:], T.m[:, 0:1], T.m[:, 1:2], MAX, MAX).then_inc(S.vb, 1)
     P.wait_ge(S.ci, 1)
-    P.wait_ge(S.vb, 1)
-    P.matmul(T.pt[:, 0:NC], T.mb[:], T.ident[:], True, True).then_inc(S.tp, 1)
-    V.wait_ge(S.tp, 1)
-    V.tensor_reduce(col(OWN), T.pt[:, 0:NC], AxisListType.X, MAX).then_inc(S.own, 1)
+    over_partitions(col(OWN), [m0, m1], T.mb, T.pb, S.vb, S.tb, S.own)
+    if to_ahead:
+        over_partitions(col(FIRST), [m1], T.mc, T.pc, S.vc, S.tc, S.late)
 
     def to_peers(which):
         if which:
-            send([(col(OWN), peer_sem(q, rank), [(cores[q], col(OWN + columns(T, topo, q).index(rank)))]) for q in which], "left")
+            send([(col(OWN), peer_sem(q, rank), [(cores[q], col(FIRST + columns(T, topo, q).index(rank)))]) for q in which], "left")
 
     def to_other_rack(single):
         groups = {}
         for q in range(n):
-            at = OWN + len(columns(T, topo, q))
+            at = FIRST + len(columns(T, topo, q))
             if rack_of(topo, cores[q]) == rack_of(topo, core):
                 continue
             for s, k in across(T, topo, q):
@@ -197,62 +233,87 @@ def rank_program(g, core, T, topo):
                     groups.setdefault(k, []).append((cores[q], col(at, k)))
                 at += k
         for k in groups:
+            if to_ahead:
+                g.wait_ge(S.late, 1)
             wait_peers(g, mine[1:k])
-            send([(col(OWN, k), S.cross, groups[k])], "left")
+            send([(col(FIRST, k), S.cross, groups[k])], "left")
 
+    if to_ahead:
+        g.wait_ge(S.vm0, 1)
+        dests = []
+        for q in to_ahead:
+            i = [r for r in range(n) if q in ahead(T, topo, r)].index(rank)
+            dests.append((cores[q], T.ah[:, i:i + 1]))
+        send([(m0, S.ahead, dests)], "left")
     g.wait_ge(S.own, 1)
     other_chip, same_chip = calls_to_peers(T, topo, rank)
     to_peers(other_chip)
-    to_other_rack(True)
     to_peers(same_chip)
+    to_other_rack(True)
     to_other_rack(False)
 
-    V.tensor_scalar(T.e[:, 0:4 * NC:4], z0, 0.0, None, MAX).then_inc(S.ev, 1)
-    V.tensor_scalar(T.e[:, 1:4 * NC:4], z0, -1.0, 0.0, MULT, MAX).then_inc(S.ev, 1)
+    X.wait_ge(S.vm0, 1)
     X.wait_ge(S.vm1, 1)
+    X.activation(T.e[:, 0:4 * NC:4], z0, Relu, scale=1.0).then_inc(S.es, 1)
+    X.activation(T.e[:, 1:4 * NC:4], z0, Relu, scale=-1.0).then_inc(S.es, 1)
     X.activation(T.e[:, 2:4 * NC:4], z1, Relu, scale=1.0).then_inc(S.es, 1)
     X.activation(T.e[:, 3:4 * NC:4], z1, Relu, scale=-1.0).then_inc(S.es, 1)
-    V.wait_ge(S.lw2, 16)
-    V.quantize_mx(T.qw2[:], T.sw2[:], T.w2t[:]).then_inc(S.vq2, 1)
+    if from_ahead:
+        V.wait_ge(S.ahead, sum(engines(wide(T, topo, q)) for q in from_ahead))
+        over_partitions(col(EARLY), [T.ah[:, i:i + 1] for i in range(len(from_ahead))], T.md, T.pd, S.vd, S.td, S.early)
 
-    V.wait_ge(S.ev, 2)
-    V.wait_ge(S.es, 2)
+    V.wait_ge(S.es, 4)
     V.wait_ge(S.own, 1)
+    if to_ahead:
+        V.wait_ge(S.late, 1)
+    if from_ahead:
+        V.wait_ge(S.early, 1)
     wait_peers(V, mine[1:])
     V.wait_ge(S.cross, sum(engines(wide(T, topo, q)) for q, _ in across(T, topo, rank)))
-    V.tensor_reduce(T.a[:, 0:1], col(OWN, n), AxisListType.X, MAX).then_inc(S.va, 1)
+    V.tensor_reduce(T.a[:, 0:1], col(EARLY, FIRST + n - EARLY), AxisListType.X, MAX).then_inc(S.va, 1)
     V.wait_ge(S.va, 1)
     V.reciprocal(T.s[:, 0:1], T.a[:, 0:1]).then_inc(S.vs, 1)
     V.wait_ge(S.vs, 1)
     V.tensor_scalar(T.ht[:, 0:H], T.e[:, 0:H], T.s[:, 0:1], None, MULT).then_inc(S.hv, 1)
-    X.wait_ge(S.ev, 2)
-    X.wait_ge(S.es, 2)
+    X.wait_ge(S.es, 4)
     X.wait_ge(S.vs, 1)
     X.activation(T.ht[:, H:2 * H], T.e[:, H:2 * H], Copy, scale=T.s[:, 0:1]).then_inc(S.hs, 1)
     V.wait_ge(S.hv, 1)
     V.wait_ge(S.hs, 1)
     V.quantize_mx(T.qh[:], T.sh[:], T.ht[:]).then_inc(S.vh, 1)
+    V.wait_ge(S.lw2, 16)
+    V.quantize_mx(T.qw2[:], T.sw2[:], T.w2t[:]).then_inc(S.vq2, 1)
 
+    aid = helper(T, topo, rank, reader)
     g.wait_ge(S.vh, 1)
     if via:
         first, second = cores[via[0]], cores[via[1]]
-        send([(codes(T.qh, 0, CUT), S.rel, [(first, codes(T.qr, 0, CUT))])], "lefth")
-        send([(T.sh[:, 0:NC], S.rel, [(second, T.sr[:, 0:NC])]),
-              (codes(T.qh, CUT, NC), S.rel, [(second, codes(T.qr, CUT, NC))])], "lefth")
+        send([(codes(T.qh, 0, HEAD), S.rel1, [(first, codes(T.qr, 0, HEAD))]),
+              (codes(T.qh, CUT, NC), S.rel1, [(second, codes(T.qr, CUT, NC))])], "lefth")
+        send([(codes(T.qh, HEAD, CUT), S.rel2, [(first, codes(T.qr, HEAD, CUT))]),
+              (T.sh[:, 0:NC], S.rel2, [(second, T.sr[:, 0:NC])])], "lefth")
     else:
+        if aid is not None:
+            send([(T.sh[:, 0:NC], S.help, [(cores[aid], T.sr[:, 0:NC])])], "lefth")
         send([(codes(T.qh, 0, NC), S.hin, [(cores[reader], codes(T.qn, 0, NC))])], "lefth")
-        send([(T.sh[:, 0:NC], S.hin, [(cores[reader], T.sn[:, 0:NC])])], "lefth")
+        if aid is None:
+            send([(T.sh[:, 0:NC], S.hin, [(cores[reader], T.sn[:, 0:NC])])], "lefth")
     for src in range(n):
         end = (src - 1) % n
         over = relays(T, topo, src, end)
-        if rank not in over:
-            continue
-        g.wait_ge(S.rel, engines(wide(T, topo, src)))
-        if over[0] == rank:
-            send([(codes(T.qr, 0, CUT), S.hin, [(cores[end], codes(T.qn, 0, CUT))])], "left")
-        else:
-            send([(T.sr[:, 0:NC], S.hin, [(cores[end], T.sn[:, 0:NC])]),
-                  (codes(T.qr, CUT, NC), S.hin, [(cores[end], codes(T.qn, CUT, NC))])], "left")
+        if rank in over:
+            part = engines(wide(T, topo, src)) // 2
+            g.wait_ge(S.rel1, part)
+            a, b = (0, HEAD) if over[0] == rank else (CUT, NC)
+            send([(codes(T.qr, a, b), S.hin, [(cores[end], codes(T.qn, a, b))])], "left")
+            g.wait_ge(S.rel2, part)
+            if over[0] == rank:
+                send([(codes(T.qr, HEAD, CUT), S.hin, [(cores[end], codes(T.qn, HEAD, CUT))])], "left")
+            else:
+                send([(T.sr[:, 0:NC], S.hin, [(cores[end], T.sn[:, 0:NC])])], "left")
+        if helper(T, topo, src, end) == rank:
+            g.wait_ge(S.help, engines(wide(T, topo, src)))
+            send([(T.sr[:, 0:NC], S.hin, [(cores[end], T.sn[:, 0:NC])])], "left")
 
     Y.wait_ge(S.hv, 1)
     Y.wait_ge(S.hs, 1)
@@ -264,7 +325,9 @@ def rank_program(g, core, T, topo):
     P.wait_ge(S.vh, 1)
     P.matmul_mx(T.yp[:, 0:NC], T.qw2[:, 0:NC], T.sw2[:, 0:NC], T.qh[:], T.sh[:], True, False)
     over = relays(T, topo, source, rank)
-    P.wait_ge(S.hin, sum(engines(wide(T, topo, q)) for q in over) or 2 * engines(wide(T, topo, source)))
+    who = helper(T, topo, source, rank)
+    P.wait_ge(S.hin, sum(2 * engines(wide(T, topo, q)) for q in over) or
+              engines(wide(T, topo, source)) + engines(wide(T, topo, source if who is None else who)))
     P.matmul_mx(T.yp[:, 0:NC], T.qw2[:, NC:2 * NC], T.sw2[:, NC:2 * NC], T.qn[:], T.sn[:], False, True).then_inc(S.ty, 1)
     V.wait_ge(S.ty, 1)
     V.tensor_copy(T.yt[:], T.yp[:, 0:NC]).then_inc(S.vy, 1)

from concourse.bass import DstId, RemoteDMATransfer
from concourse.mybir import dt, AluOpType, AxisListType, ActivationFunctionType

NC = 128
FIRST = 3
BANK = 512
CUT = 80
HEAD = 48

SCRATCH = {
    "xt": ("sbuf", [128, 4 * NC], "bfloat16"),
    "w1t": ("sbuf", [128, 8 * NC], "bfloat16"),
    "w2t": ("sbuf", [128, 8 * NC], "bfloat16"),
    "qx": ("sbuf", [128, NC], "float8_e4m3fn_x4"),
    "sx": ("sbuf", [128, NC], "uint8"),
    "qw1": ("sbuf", [128, 2 * NC], "float8_e4m3fn_x4"),
    "sw1": ("sbuf", [128, 2 * NC], "uint8"),
    "qw2": ("sbuf", [128, 2 * NC], "float8_e4m3fn_x4"),
    "sw2": ("sbuf", [128, 2 * NC], "uint8"),
    "zero": ("sbuf", [128, NC], "float32"),
    "one": ("sbuf", [128, NC], "float32"),
    "ident": ("sbuf", [128, NC], "float32"),
    "m": ("sbuf", [128, 8], "float32"),
    "mb": ("sbuf", [128, NC], "float32"),
    "mc": ("sbuf", [128, NC], "float32"),
    "md": ("sbuf", [128, NC], "float32"),
    "ah": ("sbuf", [128, 4], "float32"),
    "g": ("sbuf", [128, 8], "float32"),
    "a": ("sbuf", [128, 4], "float32"),
    "s": ("sbuf", [128, 4], "float32"),
    "e": ("sbuf", [128, 4 * NC], "float32"),
    "ht": ("sbuf", [128, 4 * NC], "bfloat16"),
    "qh": ("sbuf", [128, NC], "float8_e4m3fn_x4"),
    "sh": ("sbuf", [128, NC], "uint8"),
    "qn": ("sbuf", [128, NC], "float8_e4m3fn_x4"),
    "sn": ("sbuf", [128, NC], "uint8"),
    "qr": ("sbuf", [128, NC], "float8_e4m3fn_x4"),
    "sr": ("sbuf", [128, NC], "uint8"),
    "yt": ("sbuf", [128, NC], "float32"),
    "z": ("psum", [128, 2 * BANK], "float32"),
    "pb": ("psum", [128, BANK], "float32"),
    "pc": ("psum", [128, BANK], "float32"),
    "pd": ("psum", [128, BANK], "float32"),
    "yp": ("psum", [128, BANK], "float32"),
}
SEMAPHORES = ["lx", "lw0", "lw1", "lw2", "c0", "c1", "ci", "vqx", "vq0", "vq1", "vq2", "tz0", "tz1", "vm0", "vm1",
              "vb", "tb", "own", "vc", "tc", "late", "vd", "td", "early", "es", "va", "vs", "hv", "hs", "vh", "ty", "vy",
              "sth", "sty", "ahead", "peer1", "peer2", "cross", "hin", "rel1", "rel2", "help", "left", "lefth"]


def engines(mask):
    return bin(mask).count("1")


def share(mask, i, k):
    bits = [b for b in range(mask.bit_length()) if mask >> b & 1]
    return sum(1 << b for b in bits[i::k])


def rack_of(topo, core):
    return topo.rack(topo.host(core))


def columns(T, topo, r):
    cores = T.cores
    return [r] + [q for q in range(len(cores)) if q != r and rack_of(topo, cores[q]) == rack_of(topo, cores[r])]


def calls_to_peers(T, topo, r):
    cores = T.cores
    peers = columns(T, topo, r)[1:]
    away = [q for q in peers if topo.host(cores[q]) != topo.host(cores[r])]
    return [away, [q for q in peers if q not in away]]


def across(T, topo, r):
    cores = T.cores
    other = [q for q in range(len(cores)) if rack_of(topo, cores[q]) != rack_of(topo, cores[r])]
    able = [q for q in other if topo.may_write(cores[q], cores[r])]
    held = columns(T, topo, able[0])
    k = max([0] + [held.index(q) for q in other if q not in able]) + 1
    return [(able[0], k)] + [(q, 1) for q in able[1:] if q not in held[:k]]


def relays(T, topo, r, reader):
    cores = T.cores
    if topo.may_write(cores[r], cores[reader]):
        return []
    via = [q for q in range(len(cores)) if q not in (r, reader) and topo.may_write(cores[r], cores[q]) and topo.may_write(cores[q], cores[reader])]
    via.sort(key=lambda q: (rack_of(topo, cores[q]) != rack_of(topo, cores[r]), q))
    return [via[0], via[-1]]


def helper(T, topo, r, reader):
    cores = T.cores
    if relays(T, topo, r, reader) or rack_of(topo, cores[r]) == rack_of(topo, cores[reader]):
        return None
    near = [q for q in range(len(cores)) if q not in (r, reader) and topo.host(cores[q]) == topo.host(cores[r]) and topo.may_write(cores[q], cores[reader])]
    return near[0] if near else None


def targets(T, topo, r):
    return [q for q in range(len(T.cores)) if rack_of(topo, T.cores[q]) != rack_of(topo, T.cores[r]) and r in [s for s, _ in across(T, topo, q)]]


def ahead(T, topo, r):
    to = targets(T, topo, r)
    return [] if any(relays(T, topo, q, (q - 1) % len(T.cores)) for q in to) else to


def wide(T, topo, r):
    masks = [topo.mask(T.cores[r], c) for c in T.cores if c != T.cores[r] and topo.may_write(T.cores[r], c)]
    m = masks[0]
    for k in masks:
        m &= k
    return m


def rank_program(g, core, T, topo):
    rank = T.rank_of(core)
    if rank is None:
        return
    cores = T.cores
    n = len(cores)
    S = T.sem
    V, X, P, Y = g.vector, g.scalar, g.tensor, g.sync
    MAX, MULT = AluOpType.max, AluOpType.mult
    Relu, Copy = ActivationFunctionType.Relu, ActivationFunctionType.Copy
    H = 2 * NC
    left = {"left": 0, "lefth": 0}
    mask = wide(T, topo, rank)

    def send(parts, local):
        left[local] += engines(mask)
        if len(parts) == 1 and len(parts[0][2]) == 1:
            src, sem, [(d, out)] = parts[0]
            rid, pid = topo.addr(d, core)
            g.remote_dma(out, src, sem, S[local], pid, rid, mask)
            return
        ts = []
        for i, (src, sem, dests) in enumerate(parts):
            ids = []
            for d, _ in dests:
                rid, pid = topo.addr(d, core)
                ids.append(DstId(rid=rid, pnc=pid))
            ts.append(RemoteDMATransfer(dst_ids=ids, dma_engine_mask=share(mask, i, len(parts)), remote_sem=sem,
                                        srcs=[src], dsts=[out for _, out in dests]))
        g.remote_dma_fused(ts, local_sem=S[local])

    def codes(t, a, b):
        return t[:, a:b].bitcast(dt.uint8)

    def col(c, k=1):
        return T.g[:, c:c + k]

    mine = columns(T, topo, rank)
    reader = (rank - 1) % n
    source = (rank + 1) % n
    via = relays(T, topo, rank, reader)
    to_ahead = ahead(T, topo, rank)
    from_ahead = [q for q in range(n) if rank in ahead(T, topo, q)]
    OWN = FIRST - 1 if to_ahead else FIRST
    EARLY = OWN - 1 if from_ahead else OWN

    def peer_sem(r, q):
        return S["peer%d" % columns(T, topo, r).index(q)]

    def wait_peers(queue, which):
        for q in which:
            together = [len(c) for c in calls_to_peers(T, topo, q) if rank in c][0]
            queue.wait_ge(peer_sem(rank, q), engines(wide(T, topo, q)) // together)

    Y.dma_start(T.xt[:], T.x[:]).then_inc(S.lx, 16)
    X.dma_start(T.w1t[:, 0:4 * NC], T.w1[:, 0:4 * NC]).then_inc(S.lw0, 16)
    Y.dma_start(T.w1t[:, 4 * NC:8 * NC], T.w1[:, 4 * NC:8 * NC]).then_inc(S.lw1, 16)
    wait_peers(Y, mine[1:])
    Y.dma_start(T.w2t[:], T.w2[:]).then_inc(S.lw2, 16)

    V.memset(T.one[:], 1.0).then_inc(S.c1, 1)
    V.memset(T.zero[:], 0.0).then_inc(S.c0, 1)
    g.wait_ge(S.c1, 1)
    g.affine_select(T.ident[:], T.one[:], [[-1, NC]], AluOpType.is_equal, 0.0, 0, 1).then_inc(S.ci, 1)

    V.wait_ge(S.lx, 16)
    V.quantize_mx(T.qx[:], T.sx[:], T.xt[:]).then_inc(S.vqx, 1)
    V.wait_ge(S.lw0, 16)
    V.quantize_mx(T.qw1[:, 0:NC], T.sw1[:, 0:NC], T.w1t[:, 0:4 * NC]).then_inc(S.vq0, 1)
    V.wait_ge(S.lw1, 16)
    V.quantize_mx(T.qw1[:, NC:2 * NC], T.sw1[:, NC:2 * NC], T.w1t[:, 4 * NC:8 * NC]).then_inc(S.vq1, 1)
    z0, z1 = T.z[:, 0:NC], T.z[:, BANK:BANK + NC]
    P.wait_ge(S.vqx, 1)
    P.wait_ge(S.vq0, 1)
    P.matmul_mx(z0, T.qw1[:, 0:NC], T.sw1[:, 0:NC], T.qx[:], T.sx[:], True, True).then_inc(S.tz0, 1)
    P.wait_ge(S.vq1, 1)
    P.matmul_mx(z1, T.qw1[:, NC:2 * NC], T.sw1[:, NC:2 * NC], T.qx[:], T.sx[:], True, True).then_inc(S.tz1, 1)

    m0, m1 = T.m[:, 0:1], T.m[:, 4:5]
    V.wait_ge(S.tz0, 1)
    V.tensor_reduce(m0, z0, AxisListType.X, MAX, apply_absolute_value=True).then_inc(S.vm0, 1)
    V.wait_ge(S.tz1, 1)
    V.tensor_reduce(m1, z1, AxisListType.X, MAX, apply_absolute_value=True).then_inc(S.vm1, 1)

    def over_partitions(out, parts, spread, turned, v, t, done, meanwhile=None):
        if len(parts) == 2:
            V.tensor_scalar(spread[:], T.zero[:], parts[0], parts[1], MAX, MAX).then_inc(v, 1)
        else:
            V.tensor_scalar(spread[:], T.zero[:], parts[0], None, MAX).then_inc(v, 1)
        P.wait_ge(v, 1)
        P.matmul(turned[:, 0:NC], spread[:], T.ident[:], True, True).then_inc(t, 1)
        V.wait_ge(t, 1)
        V.tensor_reduce(out, turned[:, 0:NC], AxisListType.X, MAX).then_inc(done, 1)

    V.wait_ge(S.c0, 1)
    V.wait_ge(S.vm0, 1)
    V.wait_ge(S.vm1, 1)
    P.wait_ge(S.ci, 1)
    over_partitions(col(OWN), [m0, m1], T.mb, T.pb, S.vb, S.tb, S.own)
    if to_ahead:
        over_partitions(col(FIRST), [m1], T.mc, T.pc, S.vc, S.tc, S.late)

    def to_peers(which):
        if which:
            send([(col(OWN), peer_sem(q, rank), [(cores[q], col(FIRST + columns(T, topo, q).index(rank)))]) for q in which], "left")

    def to_other_rack(single):
        groups = {}
        for q in range(n):
            at = FIRST + len(columns(T, topo, q))
            if rack_of(topo, cores[q]) == rack_of(topo, core):
                continue
            for s, k in across(T, topo, q):
                if s == rank and (k == 1) == single:
                    groups.setdefault(k, []).append((cores[q], col(at, k)))
                at += k
        for k in groups:
            if to_ahead:
                g.wait_ge(S.late, 1)
            wait_peers(g, mine[1:k])
            send([(col(FIRST, k), S.cross, groups[k])], "left")

    if to_ahead:
        g.wait_ge(S.vm0, 1)
        dests = []
        for q in to_ahead:
            i = [r for r in range(n) if q in ahead(T, topo, r)].index(rank)
            dests.append((cores[q], T.ah[:, i:i + 1]))
        send([(m0, S.ahead, dests)], "left")
    g.wait_ge(S.own, 1)
    other_chip, same_chip = calls_to_peers(T, topo, rank)
    to_peers(other_chip)
    to_peers(same_chip)
    to_other_rack(True)
    to_other_rack(False)

    X.wait_ge(S.vm0, 1)
    X.wait_ge(S.vm1, 1)
    X.activation(T.e[:, 0:4 * NC:4], z0, Relu, scale=1.0).then_inc(S.es, 1)
    X.activation(T.e[:, 1:4 * NC:4], z0, Relu, scale=-1.0).then_inc(S.es, 1)
    X.activation(T.e[:, 2:4 * NC:4], z1, Relu, scale=1.0).then_inc(S.es, 1)
    X.activation(T.e[:, 3:4 * NC:4], z1, Relu, scale=-1.0).then_inc(S.es, 1)
    if from_ahead:
        V.wait_ge(S.ahead, sum(engines(wide(T, topo, q)) for q in from_ahead))
        over_partitions(col(EARLY), [T.ah[:, i:i + 1] for i in range(len(from_ahead))], T.md, T.pd, S.vd, S.td, S.early)

    V.wait_ge(S.es, 4)
    V.wait_ge(S.own, 1)
    if to_ahead:
        V.wait_ge(S.late, 1)
    if from_ahead:
        V.wait_ge(S.early, 1)
    wait_peers(V, mine[1:])
    V.wait_ge(S.cross, sum(engines(wide(T, topo, q)) for q, _ in across(T, topo, rank)))
    V.tensor_reduce(T.a[:, 0:1], col(EARLY, FIRST + n - EARLY), AxisListType.X, MAX).then_inc(S.va, 1)
    V.wait_ge(S.va, 1)
    V.reciprocal(T.s[:, 0:1], T.a[:, 0:1]).then_inc(S.vs, 1)
    V.wait_ge(S.vs, 1)
    V.tensor_scalar(T.ht[:, 0:H], T.e[:, 0:H], T.s[:, 0:1], None, MULT).then_inc(S.hv, 1)
    X.wait_ge(S.es, 4)
    X.wait_ge(S.vs, 1)
    X.activation(T.ht[:, H:2 * H], T.e[:, H:2 * H], Copy, scale=T.s[:, 0:1]).then_inc(S.hs, 1)
    V.wait_ge(S.hv, 1)
    V.wait_ge(S.hs, 1)
    V.quantize_mx(T.qh[:], T.sh[:], T.ht[:]).then_inc(S.vh, 1)
    V.wait_ge(S.lw2, 16)
    V.quantize_mx(T.qw2[:], T.sw2[:], T.w2t[:]).then_inc(S.vq2, 1)

    aid = helper(T, topo, rank, reader)
    g.wait_ge(S.vh, 1)
    if via:
        first, second = cores[via[0]], cores[via[1]]
        send([(codes(T.qh, 0, HEAD), S.rel1, [(first, codes(T.qr, 0, HEAD))]),
              (codes(T.qh, CUT, NC), S.rel1, [(second, codes(T.qr, CUT, NC))])], "lefth")
        send([(codes(T.qh, HEAD, CUT), S.rel2, [(first, codes(T.qr, HEAD, CUT))]),
              (T.sh[:, 0:NC], S.rel2, [(second, T.sr[:, 0:NC])])], "lefth")
    else:
        if aid is not None:
            send([(T.sh[:, 0:NC], S.help, [(cores[aid], T.sr[:, 0:NC])])], "lefth")
        send([(codes(T.qh, 0, NC), S.hin, [(cores[reader], codes(T.qn, 0, NC))])], "lefth")
        if aid is None:
            send([(T.sh[:, 0:NC], S.hin, [(cores[reader], T.sn[:, 0:NC])])], "lefth")
    for src in range(n):
        end = (src - 1) % n
        over = relays(T, topo, src, end)
        if rank in over:
            part = engines(wide(T, topo, src)) // 2
            g.wait_ge(S.rel1, part)
            a, b = (0, HEAD) if over[0] == rank else (CUT, NC)
            send([(codes(T.qr, a, b), S.hin, [(cores[end], codes(T.qn, a, b))])], "left")
            g.wait_ge(S.rel2, part)
            if over[0] == rank:
                send([(codes(T.qr, HEAD, CUT), S.hin, [(cores[end], codes(T.qn, HEAD, CUT))])], "left")
            else:
                send([(T.sr[:, 0:NC], S.hin, [(cores[end], T.sn[:, 0:NC])])], "left")
        if helper(T, topo, src, end) == rank:
            g.wait_ge(S.help, engines(wide(T, topo, src)))
            send([(T.sr[:, 0:NC], S.hin, [(cores[end], T.sn[:, 0:NC])])], "left")

    Y.wait_ge(S.hv, 1)
    Y.wait_ge(S.hs, 1)
    if via:
        Y.wait_ge(S.lefth, left["lefth"])
    Y.dma_start(T.h[:], T.ht[:]).then_inc(S.sth, 16)

    P.wait_ge(S.vq2, 1)
    P.wait_ge(S.vh, 1)
    P.matmul_mx(T.yp[:, 0:NC], T.qw2[:, 0:NC], T.sw2[:, 0:NC], T.qh[:], T.sh[:], True, False)
    over = relays(T, topo, source, rank)
    who = helper(T, topo, source, rank)
    P.wait_ge(S.hin, sum(2 * engines(wide(T, topo, q)) for q in over) or
              engines(wide(T, topo, source)) + engines(wide(T, topo, source if who is None else who)))
    P.matmul_mx(T.yp[:, 0:NC], T.qw2[:, NC:2 * NC], T.sw2[:, NC:2 * NC], T.qn[:], T.sn[:], False, True).then_inc(S.ty, 1)
    V.wait_ge(S.ty, 1)
    V.tensor_copy(T.yt[:], T.yp[:, 0:NC]).then_inc(S.vy, 1)
    Y.wait_ge(S.vy, 1)
    Y.dma_start(T.y[:], T.yt[:]).then_inc(S.sty, 16)

    g.wait_ge(S.left, left["left"])
    g.wait_ge(S.lefth, left["lefth"])
    Y.wait_ge(S.sth, 16)
    Y.wait_ge(S.sty, 16)
